import numpy as np
import ml_dtypes


def mxq(x, axis, fmt="e4m3"):
    dtype, down = {"e4m3": (ml_dtypes.float8_e4m3fn, 7), "e5m2": (ml_dtypes.float8_e5m2, 14)}[fmt]
    v = np.moveaxis(np.asarray(x, np.float32).astype(ml_dtypes.bfloat16).astype(np.float64), axis, -1)
    blocks = v.reshape(v.shape[:-1] + (-1, 32))
    amax = np.abs(blocks).max(-1, keepdims=True)
    byte = np.maximum(np.where(amax > 0, np.frexp(amax)[1] - 1 + 127, 0) - down, 1)
    scale = np.exp2(byte - 127.0)
    codes = (blocks / scale).astype(np.float32).astype(dtype).astype(np.float64)
    return np.moveaxis((codes * scale).reshape(v.shape), -1, axis)


WIDE = False


def mx_kscale(k):
    if not WIDE:
        return np.ones(k)
    levels = np.array([10, -10, 5, -5, 0])
    if k % 512:
        return np.exp2(np.random.permutation(np.resize(levels, k // 32))).repeat(32)
    a = np.empty((k // 512, 16))
    for p in range(k // 512):
        a[p, :8] = np.random.permutation(np.resize(levels, 8))
        for g in range(8):
            far = levels[np.abs(levels - a[p, g]) >= 10]
            a[p, g + 8] = far[np.random.randint(len(far))]
    return np.exp2(a.ravel()).repeat(32)


def f64(x):
    return np.asarray(x).astype(np.float64)


def striped(idx):
    return np.tile(idx.reshape(-1, 16).T, (8, 1)).astype(np.uint16)


def unstriped(offs):
    return offs[:16].T.reshape(-1).astype(np.int64)


E2M1 = np.array([0.0, 0.5, 1.0, 1.5, 2.0, 3.0, 4.0, 6.0, -0.0, -0.5, -1.0, -1.5, -2.0, -3.0, -4.0, -6.0])


def pack_weight(w, fmt):
    k, n = w.shape
    w = f64(np.asarray(w, np.float32).astype(ml_dtypes.bfloat16)).reshape(k // 32, 32, n)
    amax = np.abs(w).max(1)
    if fmt == "e4m3":
        byte = np.frexp(amax)[1] - 1 + 127 - 7
    else:
        mant, ex = np.frexp(amax / 6.0)
        byte = np.where(mant > 0.5, ex, ex - 1) + 127
    byte = np.clip(np.where(amax > 0, byte, 1), 1, 254)
    scaled = (w * np.exp2(127.0 - byte)[:, None, :]).reshape(k, n).astype(np.float32)
    by_word = np.ascontiguousarray(scaled.reshape(k // 512, 128, 4, n).transpose(0, 1, 3, 2))
    if fmt == "e4m3":
        words = by_word.astype(ml_dtypes.float8_e4m3fn).view(np.uint8)
    else:
        c = by_word.astype(ml_dtypes.float4_e2m1fn).view(np.uint8) & 0xF
        words = (c[..., 0::2] | (c[..., 1::2] << 4)).reshape(k // 512, 128, 2 * n)
    return np.ascontiguousarray(words), np.ascontiguousarray(byte.astype(np.uint8).reshape(k // 512, 16, n))


def unpack_weight(words, scales, fmt):
    g, _, n = scales.shape
    words = np.ascontiguousarray(words).reshape(g, 128, n, -1)
    if fmt == "e4m3":
        vals = words.view(ml_dtypes.float8_e4m3fn).astype(np.float64)
    else:
        nib = np.empty((g, 128, n, 4), np.uint8)
        nib[..., 0::2] = words & 0xF
        nib[..., 1::2] = words >> 4
        vals = E2M1[nib]
    vals = vals * np.repeat(np.exp2(scales.astype(np.float64) - 127.0), 8, axis=1)[..., None]
    return vals.transpose(0, 1, 3, 2).reshape(g * 512, n)


def gelu(v):
    return 0.5 * v * (1.0 + np.tanh(np.sqrt(2.0 / np.pi) * (v + 0.044715 * v**3)))


K, K2, H, N, T, T2, S = 1024, 512, 1024, 512, 2048, 4096, 1024

def setup_inputs():
    n = np.random.standard_normal
    s = mx_kscale(K)[:, None]
    s2 = mx_kscale(K2)[:, None]
    u = mx_kscale(H)[:, None]
    tab_words, tab_scales = pack_weight(n((K, T)) * s, "e4m3")
    tab2_words, tab2_scales = pack_weight(n((K2, T2)) * s2, "e4m3")
    w1 = (n((K, H)) / np.sqrt(K) / s * u.T).astype(np.float32)
    w4_words, w4_scales = pack_weight(n((K2, H)) / np.sqrt(K2) / s2 * u.T, "e2m1")
    return {
        "tab_words": tab_words, "tab_scales": tab_scales,
        "offs": striped(np.random.permutation(T)[:S]),
        "tab2_words": tab2_words, "tab2_scales": tab2_scales,
        "offs2": striped(np.random.permutation(T2)[:S]),
        "w1": w1, "w4_words": w4_words, "w4_scales": w4_scales,
        "jump": (0.5 * n(H) * u[:, 0]).astype(np.float32),
        "cond": np.exp(0.3 * n((H, S))).astype(np.float32),
        "wf": (n((H, N)) / np.sqrt(H) / u).astype(np.float32),
        "q0": (0.5 * n(N)).astype(np.float32),
    }

def reference(tab_words, tab_scales, offs, tab2_words, tab2_scales, offs2,
              w1, w4_words, w4_scales, jump, cond, wf, q0):
    v = unpack_weight(tab_words, tab_scales, "e4m3")[:, unstriped(offs)]
    v2 = unpack_weight(tab2_words, tab2_scales, "e4m3")[:, unstriped(offs2)]
    left = mxq(f64(w1), 0, "e4m3").T @ v
    right = unpack_weight(w4_words, w4_scales, "e2m1").T @ v2
    h = (left - right + f64(jump)[:, None]) * f64(cond)
    y = mxq(f64(wf), 0, "e4m3").T @ mxq(h, 0, "e4m3")
    return y + f64(q0)[:, None]

@@ -1,0 +1,231 @@
+from contextlib import ExitStack
+
+import concourse.mybir as mybir
+
+K, K2, H, N, T, T2, S = 1024, 512, 1024, 512, 2048, 4096, 1024
+FLOPS = 2 * S * (K * H + K2 * H + H * N)
+
+F32 = mybir.dt.float32
+BF16 = mybir.dt.bfloat16
+I32 = mybir.dt.int32
+U32 = mybir.dt.uint32
+U16 = mybir.dt.uint16
+U8 = mybir.dt.uint8
+FP8X4 = mybir.dt.float8_e4m3fn_x4
+FP4X4 = mybir.dt.float4_e2m1fn_x4
+MULT = mybir.AluOpType.mult
+ADD = mybir.AluOpType.add
+COPY = mybir.ActivationFunctionType.Copy
+IDENTITY = mybir.ActivationFunctionType.Identity
+
+P = 128
+PACK = 4
+PASS = P * PACK
+BANK = 512
+CHUNKS = [(0, 256), (256, 512), (512, 768), (768, 896), (896, 1024)]
+B0_CHUNKS = [(0, 256), (256, 512), (512, 768), (768, 1024)]
+
+
+def tile_list_interface_face_flux_kernel(
+    tc, tab_words, tab_scales, offs, tab2_words, tab2_scales, offs2,
+    w1, w4_words, w4_scales, jump, cond, wf, q0, out,
+):
+    nc = tc.nc
+    with ExitStack() as ctx:
+        held = ctx.enter_context(tc.tile_pool(name="held", bufs=1))
+        ring = ctx.enter_context(tc.tile_pool(name="ring", bufs=1))
+        psum = ctx.enter_context(tc.psum_pool(name="psum", bufs=8))
+
+        def keep(shape, dtype, name):
+            return held.tile(shape, dtype, name=name, align_bytes=64)
+
+        left_list = keep([P, S // 16], U16, "left_list")
+        right_list = keep([P, S // 16], U16, "right_list")
+        left_words = [keep([P, T], I32, f"left_words{a}") for a in range(2)]
+        right_words = keep([P, T2], I32, "right_words")
+        left_scales = keep([P, T // 4], I32, "left_scales")
+        right_scales = keep([P, T2 // 4], I32, "right_scales")
+        w4_raw = keep([P, H // 2], I32, "w4_raw")
+        w4_raw_scales = keep([P, H // 4], I32, "w4_raw_scales")
+        w4_codes = keep([P, 2 * H], U8, "w4_codes")
+        w4_planes = keep([P, H], U8, "w4_planes")
+        v_codes = [keep([P, S], U32, f"v_codes{a}") for a in range(2)]
+        v_planes = keep([P, S], U8, "v_planes")
+        v2_codes = keep([P, S], U32, "v2_codes")
+        v2_planes = keep([P, S], U8, "v2_planes")
+        w1_codes = [[keep([P, PASS], U32, f"w1_codes{a}{b}") for b in range(2)] for a in range(2)]
+        w1_planes = [[keep([P, PASS], U8, f"w1_planes{a}{b}") for b in range(2)] for a in range(2)]
+        wf_raw = [keep([P, PACK, N], F32, f"wf_raw{b}") for b in range(2)]
+        wf_codes = [keep([P, N], U32, f"wf_codes{b}") for b in range(2)]
+        wf_planes = [keep([P, N], U8, f"wf_planes{b}") for b in range(2)]
+        diff = [keep([P, PACK, S], F32, f"diff{b}") for b in range(2)]
+        cond_sb = [keep([P, PACK, S], F32, f"cond{b}") for b in range(2)]
+        h_codes = [keep([P, S], U32, f"h_codes{b}") for b in range(2)]
+        h_planes = [keep([P, S], U8, f"h_planes{b}") for b in range(2)]
+        jump_sb = keep([P, 2, PACK], F32, "jump_sb")
+        q0_sb = keep([P, N // P], F32, "q0_sb")
+        w1_raw = [[ring.tile([P, PACK, PASS], F32, name=f"w1_raw{a}{b}", tag="wide", bufs=4, align_bytes=64)
+                   for b in range(2)] for a in range(2)]
+
+        nc.gpsimd.memset(left_scales[:], 0)
+        nc.vector.memset(right_scales[:], 0)
+        nc.vector.memset(w4_raw_scales[:], 0)
+
+        def load_left_scales():
+            for quad in range(4):
+                nc.sync.dma_start(left_scales[32 * quad + 4 : 32 * quad + 12, :],
+                                  tab_scales[:, 4 * quad : 4 * quad + 4, :].bitcast(I32))
+
+        def load_scales(dst, src):
+            rows = src[0].bitcast(I32).rearrange("(q r) n -> r q n", r=4)
+            for r in range(4):
+                nc.sync.dma_start(dst[r:P:32, :], rows[r])
+
+        def load_words(dst, src):
+            nc.sync.dma_start(dst[:], src.rearrange("p n i -> p (n i)").bitcast(I32))
+
+        def load_w1(a, b):
+            rows = w1[PASS * a : PASS * (a + 1), PASS * b : PASS * (b + 1)]
+            nc.sync.dma_start(w1_raw[a][b][:], rows.rearrange("(p i) c -> p i c", i=PACK))
+
+        def load_cond(b, lo, hi):
+            rows = cond[PASS * b : PASS * (b + 1), lo:hi]
+            nc.sync.dma_start(cond_sb[b][:, :, lo:hi], rows.rearrange("(p t) j -> p t j", t=PACK))
+
+        nc.sync.dma_start(left_list[:], offs)
+        load_words(left_words[0], tab_words[0])
+        nc.sync.dma_start(right_list[:], offs2)
+        nc.sync.dma_start(jump_sb[:], jump.rearrange("(b p t) -> p b t", b=2, t=PACK))
+        with nc.allow_non_contiguous_dma(reason="one value of q0 for each partition"):
+            nc.sync.dma_start(q0_sb[:], q0.rearrange("(m p) -> p m", p=P))
+        nc.sync.dma_start(w4_raw[:], w4_words[0].bitcast(I32))
+        load_w1(0, 0)
+        load_left_scales()
+        load_words(left_words[1], tab_words[1])
+        load_scales(right_scales, tab2_scales)
+        load_w1(1, 0)
+        load_scales(w4_raw_scales, w4_scales)
+        load_words(right_words, tab2_words[0])
+        load_w1(0, 1)
+        load_w1(1, 1)
+        load_cond(0, 0, BANK)
+        load_cond(0, BANK, S)
+        for b in range(2):
+            rows = wf[PASS * b : PASS * (b + 1), :]
+            nc.sync.dma_start(wf_raw[b][:], rows.rearrange("(p t) n -> p t n", t=PACK))
+        for lo, hi in CHUNKS:
+            load_cond(1, lo, hi)
+
+        def staging(name):
+            return ring.tile([P, PASS * PACK], BF16, name=name, tag="staging", bufs=3, align_bytes=64)
+
+        def round_w1(a, b, on_vector):
+            grouped = staging(f"w1_grouped{a}{b}")
+            dst = grouped[:].rearrange("p (t m i) -> p m i t", t=PACK, i=PACK)
+            src = w1_raw[a][b][:].rearrange("p i (m t) -> p m i t", t=PACK)
+            if on_vector:
+                nc.vector.tensor_scalar(dst, src, -1.0, None, MULT)
+            else:
+                nc.scalar.activation(dst, src, COPY, scale=-1.0)
+            return grouped
+
+        def round_wf(b):
+            grouped = staging(f"wf_grouped{b}")
+            dst = grouped[:].rearrange("p (c e t) -> p c t e", e=4, t=PACK)
+            src = wf_raw[b][:].rearrange("p t (c e) -> p c t e", e=4)
+            nc.scalar.activation(dst, src, COPY)
+            return grouped
+
+        def quantise(codes, planes, values):
+            nc.vector.quantize_mx(out=codes.bitcast(FP8X4), scales=planes, in_=values)
+
+        def gather(dst, window, dtype, offsets):
+            nc.vector.tensor_copy(dst, window[:].bitcast(dtype).indirect(offsets))
+
+        def project(b, half):
+            cols = slice(BANK * half, BANK * (half + 1))
+            for t in range(PACK):
+                acc = psum.tile([P, BANK], F32, name="acc", tag="acc")
+                own = slice(P * t, P * (t + 1))
+                for a in range(2):
+                    nc.tensor.matmul_mx(
+                        out=acc[:], lhsT=w1_codes[a][b][:, own].bitcast(FP8X4), lhsT_scale=w1_planes[a][b][:, own],
+                        rhs=v_codes[a][:, cols].bitcast(FP8X4), rhs_scale=v_planes[4 + 4 * a : P, cols],
+                        start=(a == 0), stop=False)
+                first = PASS * b + P * t
+                nc.tensor.matmul_mx(
+                    out=acc[:], lhsT=w4_codes[:, 2 * first : 2 * (first + P)].bitcast(FP4X4),
+                    lhsT_scale=w4_planes[:, first : first + P],
+                    rhs=v2_codes[:, cols].bitcast(FP8X4), rhs_scale=v2_planes[:, cols],
+                    start=False, stop=True)
+                nc.scalar.activation(diff[b][:, t, cols], acc[:], IDENTITY, bias=jump_sb[:, b, t : t + 1], scale=-1.0)
+
+        def form_h(b, lo, hi):
+            values = ring.tile([P, (hi - lo) * PACK], BF16, name="h_values", tag="h_values", bufs=3, align_bytes=64)
+            nc.vector.tensor_tensor(
+                values[:].rearrange("p (c e t) -> p c t e", e=4, t=PACK),
+                diff[b][:, :, lo:hi].rearrange("p t (c e) -> p c t e", e=4),
+                cond_sb[b][:, :, lo:hi].rearrange("p t (c e) -> p c t e", e=4), MULT)
+            return values
+
+        def flux(lo, hi, share):
+            staged = ring.tile([P, N // P, hi - lo], F32, name="staged", tag="wide", bufs=4, align_bytes=64)
+            for m in range(N // P):
+                acc = psum.tile([P, hi - lo], F32, name="acc", tag="acc")
+                own = slice(P * m, P * (m + 1))
+                for b in range(2):
+                    nc.tensor.matmul_mx(
+                        out=acc[:], lhsT=wf_codes[b][:, own].bitcast(FP8X4), lhsT_scale=wf_planes[b][:, own],
+                        rhs=h_codes[b][:, lo:hi].bitcast(FP8X4), rhs_scale=h_planes[b][:, lo:hi],
+                        start=(b == 0), stop=(b == 1))
+                if share and m % 2 == 1:
+                    nc.vector.tensor_scalar(staged[:, m, :], acc[:], q0_sb[:, m : m + 1], None, ADD)
+                else:
+                    nc.scalar.activation(staged[:, m, :], acc[:], IDENTITY, bias=q0_sb[:, m : m + 1], scale=1.0)
+            nc.sync.dma_start(out[:, lo:hi].rearrange("(m p) j -> p m j", p=P), staged[:])
+
+        gather(v_codes[0][:], left_words[0], U32, left_list[:])
+        grouped00 = round_w1(0, 0, False)
+        gather(v_planes[:], left_scales, U8, left_list[:])
+        gather(v_codes[1][:], left_words[1], U32, left_list[:])
+        quantise(w1_codes[0][0][:], w1_planes[0][0][:], grouped00[:])
+        grouped10 = round_w1(1, 0, False)
+        gather(v2_planes[:], right_scales, U8, right_list[:])
+        nc.vector.tensor_copy(
+            w4_codes[:].bitcast(U16).rearrange("p (b t m) -> p b m t", b=2, t=PACK),
+            w4_raw[:].bitcast(U16).rearrange("p (b m t) -> p b m t", b=2, t=PACK))
+        nc.vector.tensor_copy(
+            w4_planes[:].rearrange("p (b t m) -> p b m t", b=2, t=PACK),
+            w4_raw_scales[:].bitcast(U8).rearrange("p (b m t) -> p b m t", b=2, t=PACK))
+        quantise(w1_codes[1][0][:], w1_planes[1][0][:], grouped10[:])
+        for half in range(2):
+            gather(v2_codes[:, BANK * half : BANK * (half + 1)], right_words, U32, right_list[:, 32 * half : 32 * (half + 1)])
+        project(0, 0)
+        project(0, 1)
+        grouped01 = round_w1(0, 1, True)
+        grouped11 = round_w1(1, 1, True)
+        quantise(w1_codes[0][1][:], w1_planes[0][1][:], grouped01[:])
+        quantise(w1_codes[1][1][:], w1_planes[1][1][:], grouped11[:])
+        project(1, 0)
+        project(1, 1)
+
+        pending = None
+        for lo, hi in B0_CHUNKS:
+            values = form_h(0, lo, hi)
+            if pending is not None:
+                quantise(*pending)
+            pending = (h_codes[0][:, lo:hi], h_planes[0][:, lo:hi], values[:])
+        wf_grouped = [round_wf(b) for b in range(2)]
+        quantise(*pending)
+        for b in range(2):
+            quantise(wf_codes[b][:], wf_planes[b][:], wf_grouped[b][:])
+
+        pending = None
+        for lo, hi in CHUNKS:
+            values = form_h(1, lo, hi)
+            if pending is not None:
+                quantise(h_codes[1][:, pending[0] : pending[1]], h_planes[1][:, pending[0] : pending[1]], pending[2][:])
+                flux(pending[0], pending[1], False)
+            pending = (lo, hi, values)
+        quantise(h_codes[1][:, pending[0] : pending[1]], h_planes[1][:, pending[0] : pending[1]], pending[2][:])
+        flux(pending[0], pending[1], True)

@@ -92,48 +92,58 @@ def tile_list_interface_face_flux_kernel(
             rows = cond[PASS * b : PASS * (b + 1), lo:hi]
             nc.sync.dma_start(cond_sb[b][:, :, lo:hi], rows.rearrange("(p t) j -> p t j", t=PACK))
 
-        nc.sync.dma_start(left_list[:], offs)
+        def load_wf(b):
+            rows = wf[PASS * b : PASS * (b + 1), :]
+            nc.sync.dma_start(wf_raw[b][:], rows.rearrange("(p t) n -> p t n", t=PACK))
+
         load_words(left_words[0], tab_words[0])
+        nc.sync.dma_start(left_list[:], offs)
+        nc.sync.dma_start(w4_raw[:], w4_words[0].bitcast(I32))
         nc.sync.dma_start(right_list[:], offs2)
         nc.sync.dma_start(jump_sb[:], jump.rearrange("(b p t) -> p b t", b=2, t=PACK))
         with nc.allow_non_contiguous_dma(reason="one value of q0 for each partition"):
             nc.sync.dma_start(q0_sb[:], q0.rearrange("(m p) -> p m", p=P))
-        nc.sync.dma_start(w4_raw[:], w4_words[0].bitcast(I32))
         load_w1(0, 0)
         load_left_scales()
         load_words(left_words[1], tab_words[1])
+        load_scales(w4_raw_scales, w4_scales)
         load_scales(right_scales, tab2_scales)
         load_w1(1, 0)
-        load_scales(w4_raw_scales, w4_scales)
         load_words(right_words, tab2_words[0])
         load_w1(0, 1)
         load_w1(1, 1)
-        load_cond(0, 0, BANK)
-        load_cond(0, BANK, S)
-        for b in range(2):
-            rows = wf[PASS * b : PASS * (b + 1), :]
-            nc.sync.dma_start(wf_raw[b][:], rows.rearrange("(p t) n -> p t n", t=PACK))
-        for lo, hi in CHUNKS:
-            load_cond(1, lo, hi)
+        load_cond(0, 0, 512)
+        load_wf(0)
+        load_cond(1, 0, 512)
+        load_wf(1)
+        load_cond(0, 512, 768)
+        load_cond(1, 512, 768)
+        load_cond(0, 768, 1024)
+        load_cond(1, 768, 896)
+        load_cond(1, 896, 1024)
 
         def staging(name):
             return ring.tile([P, PASS * PACK], BF16, name=name, tag="staging", bufs=3, align_bytes=64)
 
-        def round_w1(a, b, on_vector):
+        def round_w1(a, b, vector_share):
             grouped = staging(f"w1_grouped{a}{b}")
             dst = grouped[:].rearrange("p (t m i) -> p m i t", t=PACK, i=PACK)
             src = w1_raw[a][b][:].rearrange("p i (m t) -> p m i t", t=PACK)
-            if on_vector:
-                nc.vector.tensor_scalar(dst, src, -1.0, None, MULT)
-            else:
-                nc.scalar.activation(dst, src, COPY, scale=-1.0)
+            if vector_share > 0:
+                nc.vector.tensor_scalar(dst[:, :vector_share], src[:, :vector_share], -1.0, None, MULT)
+            if vector_share < P:
+                nc.scalar.activation(dst[:, vector_share:], src[:, vector_share:], COPY, scale=-1.0)
             return grouped
 
-        def round_wf(b):
+        def round_wf(b, on_vector):
             grouped = staging(f"wf_grouped{b}")
             dst = grouped[:].rearrange("p (c e t) -> p c t e", e=4, t=PACK)
             src = wf_raw[b][:].rearrange("p t (c e) -> p c t e", e=4)
-            nc.scalar.activation(dst, src, COPY)
+            for lo in (0, 64):
+                if on_vector:
+                    nc.vector.tensor_copy(dst[:, lo : lo + 64], src[:, lo : lo + 64])
+                else:
+                    nc.scalar.activation(dst[:, lo : lo + 64], src[:, lo : lo + 64], COPY)
             return grouped
 
         def quantise(codes, planes, values):
@@ -184,48 +194,51 @@ def tile_list_interface_face_flux_kernel(
                     nc.scalar.activation(staged[:, m, :], acc[:], IDENTITY, bias=q0_sb[:, m : m + 1], scale=1.0)
             nc.sync.dma_start(out[:, lo:hi].rearrange("(m p) j -> p m j", p=P), staged[:])
 
-        gather(v_codes[0][:], left_words[0], U32, left_list[:])
-        grouped00 = round_w1(0, 0, False)
-        gather(v_planes[:], left_scales, U8, left_list[:])
-        gather(v_codes[1][:], left_words[1], U32, left_list[:])
-        quantise(w1_codes[0][0][:], w1_planes[0][0][:], grouped00[:])
-        grouped10 = round_w1(1, 0, False)
-        gather(v2_planes[:], right_scales, U8, right_list[:])
         nc.vector.tensor_copy(
             w4_codes[:].bitcast(U16).rearrange("p (b t m) -> p b m t", b=2, t=PACK),
             w4_raw[:].bitcast(U16).rearrange("p (b m t) -> p b m t", b=2, t=PACK))
+        grouped00 = round_w1(0, 0, 64)
+        quantise(w1_codes[0][0][:], w1_planes[0][0][:], grouped00[:])
+        grouped10 = round_w1(1, 0, 64)
+        gather(v_codes[0][:], left_words[0], U32, left_list[:])
+        quantise(w1_codes[1][0][:], w1_planes[1][0][:], grouped10[:])
+        gather(v_planes[:], left_scales, U8, left_list[:])
+        gather(v_codes[1][:], left_words[1], U32, left_list[:])
         nc.vector.tensor_copy(
             w4_planes[:].rearrange("p (b t m) -> p b m t", b=2, t=PACK),
             w4_raw_scales[:].bitcast(U8).rearrange("p (b m t) -> p b m t", b=2, t=PACK))
-        quantise(w1_codes[1][0][:], w1_planes[1][0][:], grouped10[:])
+        gather(v2_planes[:], right_scales, U8, right_list[:])
         for half in range(2):
             gather(v2_codes[:, BANK * half : BANK * (half + 1)], right_words, U32, right_list[:, 32 * half : 32 * (half + 1)])
         project(0, 0)
         project(0, 1)
-        grouped01 = round_w1(0, 1, True)
-        grouped11 = round_w1(1, 1, True)
+        grouped01 = round_w1(0, 1, P)
+        grouped11 = round_w1(1, 1, P)
         quantise(w1_codes[0][1][:], w1_planes[0][1][:], grouped01[:])
         quantise(w1_codes[1][1][:], w1_planes[1][1][:], grouped11[:])
         project(1, 0)
         project(1, 1)
 
+        order = [(0, 0), (0, 1), (1, 0), (1, 1)] + [(b, c) for c in range(2, len(CHUNKS)) for b in range(2)]
         pending = None
-        for lo, hi in B0_CHUNKS:
-            values = form_h(0, lo, hi)
+        done = []
+        for step, (b, c) in enumerate(order + [(None, None)]):
+            if b is not None:
+                values = form_h(b, *CHUNKS[c])
             if pending is not None:
-                quantise(*pending)
-            pending = (h_codes[0][:, lo:hi], h_planes[0][:, lo:hi], values[:])
-        wf_grouped = [round_wf(b) for b in range(2)]
-        quantise(*pending)
-        for b in range(2):
-            quantise(wf_codes[b][:], wf_planes[b][:], wf_grouped[b][:])
-
-        pending = None
-        for lo, hi in CHUNKS:
-            values = form_h(1, lo, hi)
-            if pending is not None:
-                quantise(h_codes[1][:, pending[0] : pending[1]], h_planes[1][:, pending[0] : pending[1]], pending[2][:])
-                flux(pending[0], pending[1], False)
-            pending = (lo, hi, values)
-        quantise(h_codes[1][:, pending[0] : pending[1]], h_planes[1][:, pending[0] : pending[1]], pending[2][:])
-        flux(pending[0], pending[1], True)
+                pb, pc, pv = pending
+                lo, hi = CHUNKS[pc]
+                quantise(h_codes[pb][:, lo:hi], h_planes[pb][:, lo:hi], pv[:])
+                if pb == 1:
+                    done.append(pc)
+            if step == 4:
+                wf_grouped = [round_wf(0, True), round_wf(1, False)]
+                for wb in range(2):
+                    for lo in (0, 256):
+                        quantise(wf_codes[wb][:, lo : lo + 256], wf_planes[wb][:, lo : lo + 256],
+                                 wf_grouped[wb][:, PACK * lo : PACK * (lo + 256)])
+            if step >= 4:
+                for dc in done:
+                    flux(*CHUNKS[dc], dc == len(CHUNKS) - 1)
+                done = []
+            pending = (b, c, values)

@@ -73,13 +73,13 @@ def tile_list_interface_face_flux_kernel(
 
         def load_left_scales():
             for quad in range(4):
-                nc.sync.dma_start(left_scales[32 * quad + 4 : 32 * quad + 12, :],
+                nc.gpsimd.dma_start(left_scales[32 * quad + 4 : 32 * quad + 12, :],
                                   tab_scales[:, 4 * quad : 4 * quad + 4, :].bitcast(I32))
 
         def load_scales(dst, src):
             rows = src[0].bitcast(I32).rearrange("(q r) n -> r q n", r=4)
             for r in range(4):
-                nc.sync.dma_start(dst[r:P:32, :], rows[r])
+                nc.gpsimd.dma_start(dst[r:P:32, :], rows[r])
 
         def load_words(dst, src):
             nc.sync.dma_start(dst[:], src.rearrange("p n i -> p (n i)").bitcast(I32))
@@ -96,18 +96,19 @@ def tile_list_interface_face_flux_kernel(
             rows = wf[PASS * b : PASS * (b + 1), :]
             nc.sync.dma_start(wf_raw[b][:], rows.rearrange("(p t) n -> p t n", t=PACK))
 
+        load_left_scales()
+        load_scales(right_scales, tab2_scales)
+        load_scales(w4_raw_scales, w4_scales)
+        with nc.allow_non_contiguous_dma(reason="one value of q0 for each partition"):
+            nc.gpsimd.dma_start(q0_sb[:], q0.rearrange("(m p) -> p m", p=P))
+
         load_words(left_words[0], tab_words[0])
         nc.sync.dma_start(left_list[:], offs)
-        nc.sync.dma_start(w4_raw[:], w4_words[0].bitcast(I32))
         nc.sync.dma_start(right_list[:], offs2)
         nc.sync.dma_start(jump_sb[:], jump.rearrange("(b p t) -> p b t", b=2, t=PACK))
-        with nc.allow_non_contiguous_dma(reason="one value of q0 for each partition"):
-            nc.sync.dma_start(q0_sb[:], q0.rearrange("(m p) -> p m", p=P))
-        load_w1(0, 0)
-        load_left_scales()
+        nc.sync.dma_start(w4_raw[:], w4_words[0].bitcast(I32))
         load_words(left_words[1], tab_words[1])
-        load_scales(w4_raw_scales, w4_scales)
-        load_scales(right_scales, tab2_scales)
+        load_w1(0, 0)
         load_w1(1, 0)
         load_words(right_words, tab2_words[0])
         load_w1(0, 1)
@@ -135,12 +136,12 @@ def tile_list_interface_face_flux_kernel(
                 nc.scalar.activation(dst[:, vector_share:], src[:, vector_share:], COPY, scale=-1.0)
             return grouped
 
-        def round_wf(b, on_vector):
+        def round_wf(b, vector_halves):
             grouped = staging(f"wf_grouped{b}")
             dst = grouped[:].rearrange("p (c e t) -> p c t e", e=4, t=PACK)
             src = wf_raw[b][:].rearrange("p t (c e) -> p c t e", e=4)
             for lo in (0, 64):
-                if on_vector:
+                if lo in vector_halves:
                     nc.vector.tensor_copy(dst[:, lo : lo + 64], src[:, lo : lo + 64])
                 else:
                     nc.scalar.activation(dst[:, lo : lo + 64], src[:, lo : lo + 64], COPY)
@@ -194,29 +195,30 @@ def tile_list_interface_face_flux_kernel(
                     nc.scalar.activation(staged[:, m, :], acc[:], IDENTITY, bias=q0_sb[:, m : m + 1], scale=1.0)
             nc.sync.dma_start(out[:, lo:hi].rearrange("(m p) j -> p m j", p=P), staged[:])
 
+        gather(v_codes[0][:], left_words[0], U32, left_list[:])
         nc.vector.tensor_copy(
             w4_codes[:].bitcast(U16).rearrange("p (b t m) -> p b m t", b=2, t=PACK),
             w4_raw[:].bitcast(U16).rearrange("p (b m t) -> p b m t", b=2, t=PACK))
-        grouped00 = round_w1(0, 0, 64)
-        quantise(w1_codes[0][0][:], w1_planes[0][0][:], grouped00[:])
-        grouped10 = round_w1(1, 0, 64)
-        gather(v_codes[0][:], left_words[0], U32, left_list[:])
-        quantise(w1_codes[1][0][:], w1_planes[1][0][:], grouped10[:])
         gather(v_planes[:], left_scales, U8, left_list[:])
         gather(v_codes[1][:], left_words[1], U32, left_list[:])
+        gather(v2_planes[:], right_scales, U8, right_list[:])
+        grouped00 = round_w1(0, 0, 0)
+        grouped10 = round_w1(1, 0, 0)
+        quantise(w1_codes[0][0][:], w1_planes[0][0][:], grouped00[:])
+        quantise(w1_codes[1][0][:], w1_planes[1][0][:], grouped10[:])
         nc.vector.tensor_copy(
             w4_planes[:].rearrange("p (b t m) -> p b m t", b=2, t=PACK),
             w4_raw_scales[:].bitcast(U8).rearrange("p (b m t) -> p b m t", b=2, t=PACK))
-        gather(v2_planes[:], right_scales, U8, right_list[:])
         for half in range(2):
             gather(v2_codes[:, BANK * half : BANK * (half + 1)], right_words, U32, right_list[:, 32 * half : 32 * (half + 1)])
         project(0, 0)
         project(0, 1)
-        grouped01 = round_w1(0, 1, P)
+        grouped01 = round_w1(0, 1, 64)
         grouped11 = round_w1(1, 1, P)
         quantise(w1_codes[0][1][:], w1_planes[0][1][:], grouped01[:])
         quantise(w1_codes[1][1][:], w1_planes[1][1][:], grouped11[:])
         project(1, 0)
+        wf_grouped = [round_wf(0, [0]), round_wf(1, [])]
         project(1, 1)
 
         order = [(0, 0), (0, 1), (1, 0), (1, 1)] + [(b, c) for c in range(2, len(CHUNKS)) for b in range(2)]
@@ -232,7 +234,6 @@ def tile_list_interface_face_flux_kernel(
                 if pb == 1:
                     done.append(pc)
             if step == 4:
-                wf_grouped = [round_wf(0, True), round_wf(1, False)]
                 for wb in range(2):
                     for lo in (0, 256):
                         quantise(wf_codes[wb][:, lo : lo + 256], wf_planes[wb][:, lo : lo + 256],

@@ -58,13 +58,13 @@ def tile_list_interface_face_flux_kernel(
         wf_raw = [keep([P, PACK, N], F32, f"wf_raw{b}") for b in range(2)]
         wf_codes = [keep([P, N], U32, f"wf_codes{b}") for b in range(2)]
         wf_planes = [keep([P, N], U8, f"wf_planes{b}") for b in range(2)]
-        diff = [keep([P, PACK, S], F32, f"diff{b}") for b in range(2)]
-        cond_sb = [keep([P, PACK, S], F32, f"cond{b}") for b in range(2)]
+        diff = [[keep([P, PACK, BANK], F32, f"diff{b}{half}") for half in range(2)] for b in range(2)]
+        cond_sb = {}
         h_codes = [keep([P, S], U32, f"h_codes{b}") for b in range(2)]
         h_planes = [keep([P, S], U8, f"h_planes{b}") for b in range(2)]
         jump_sb = keep([P, 2, PACK], F32, "jump_sb")
         q0_sb = keep([P, N // P], F32, "q0_sb")
-        w1_raw = [[ring.tile([P, PACK, PASS], F32, name=f"w1_raw{a}{b}", tag="wide", bufs=4, align_bytes=64)
+        w1_raw = [[ring.tile([P, PACK, PASS], F32, name=f"w1_raw{a}{b}", tag="wide", bufs=5, align_bytes=64)
                    for b in range(2)] for a in range(2)]
 
         nc.gpsimd.memset(left_scales[:], 0)
@@ -73,13 +73,13 @@ def tile_list_interface_face_flux_kernel(
 
         def load_left_scales():
             for quad in range(4):
-                nc.gpsimd.dma_start(left_scales[32 * quad + 4 : 32 * quad + 12, :],
+                nc.sync.dma_start(left_scales[32 * quad + 4 : 32 * quad + 12, :],
                                   tab_scales[:, 4 * quad : 4 * quad + 4, :].bitcast(I32))
 
         def load_scales(dst, src):
             rows = src[0].bitcast(I32).rearrange("(q r) n -> r q n", r=4)
             for r in range(4):
-                nc.gpsimd.dma_start(dst[r:P:32, :], rows[r])
+                nc.sync.dma_start(dst[r:P:32, :], rows[r])
 
         def load_words(dst, src):
             nc.sync.dma_start(dst[:], src.rearrange("p n i -> p (n i)").bitcast(I32))
@@ -90,25 +90,25 @@ def tile_list_interface_face_flux_kernel(
 
         def load_cond(b, lo, hi):
             rows = cond[PASS * b : PASS * (b + 1), lo:hi]
-            nc.sync.dma_start(cond_sb[b][:, :, lo:hi], rows.rearrange("(p t) j -> p t j", t=PACK))
+            cond_sb[b, lo, hi] = keep([P, PACK, hi - lo], F32, f"cond{b}_{lo}")
+            nc.sync.dma_start(cond_sb[b, lo, hi][:], rows.rearrange("(p t) j -> p t j", t=PACK))
 
         def load_wf(b):
             rows = wf[PASS * b : PASS * (b + 1), :]
             nc.sync.dma_start(wf_raw[b][:], rows.rearrange("(p t) n -> p t n", t=PACK))
 
-        load_left_scales()
-        load_scales(right_scales, tab2_scales)
-        load_scales(w4_raw_scales, w4_scales)
-        with nc.allow_non_contiguous_dma(reason="one value of q0 for each partition"):
-            nc.gpsimd.dma_start(q0_sb[:], q0.rearrange("(m p) -> p m", p=P))
-
         load_words(left_words[0], tab_words[0])
         nc.sync.dma_start(left_list[:], offs)
+        nc.sync.dma_start(w4_raw[:], w4_words[0].bitcast(I32))
         nc.sync.dma_start(right_list[:], offs2)
         nc.sync.dma_start(jump_sb[:], jump.rearrange("(b p t) -> p b t", b=2, t=PACK))
-        nc.sync.dma_start(w4_raw[:], w4_words[0].bitcast(I32))
-        load_words(left_words[1], tab_words[1])
+        with nc.allow_non_contiguous_dma(reason="one value of q0 for each partition"):
+            nc.sync.dma_start(q0_sb[:], q0.rearrange("(m p) -> p m", p=P))
         load_w1(0, 0)
+        load_left_scales()
+        load_words(left_words[1], tab_words[1])
+        load_scales(w4_raw_scales, w4_scales)
+        load_scales(right_scales, tab2_scales)
         load_w1(1, 0)
         load_words(right_words, tab2_words[0])
         load_w1(0, 1)
@@ -126,25 +126,26 @@ def tile_list_interface_face_flux_kernel(
         def staging(name):
             return ring.tile([P, PASS * PACK], BF16, name=name, tag="staging", bufs=3, align_bytes=64)
 
-        def round_w1(a, b, vector_share):
+        def round_w1(a, b, vector_pairs):
             grouped = staging(f"w1_grouped{a}{b}")
             dst = grouped[:].rearrange("p (t m i) -> p m i t", t=PACK, i=PACK)
             src = w1_raw[a][b][:].rearrange("p i (m t) -> p m i t", t=PACK)
-            if vector_share > 0:
-                nc.vector.tensor_scalar(dst[:, :vector_share], src[:, :vector_share], -1.0, None, MULT)
-            if vector_share < P:
-                nc.scalar.activation(dst[:, vector_share:], src[:, vector_share:], COPY, scale=-1.0)
+            for t in (0, 2):
+                if t in vector_pairs:
+                    nc.vector.tensor_scalar(dst[:, :, :, t : t + 2], src[:, :, :, t : t + 2], -1.0, None, MULT)
+                else:
+                    nc.scalar.activation(dst[:, :, :, t : t + 2], src[:, :, :, t : t + 2], COPY, scale=-1.0)
             return grouped
 
         def round_wf(b, vector_halves):
             grouped = staging(f"wf_grouped{b}")
-            dst = grouped[:].rearrange("p (c e t) -> p c t e", e=4, t=PACK)
-            src = wf_raw[b][:].rearrange("p t (c e) -> p c t e", e=4)
-            for lo in (0, 64):
+            dst = grouped[:].rearrange("p (c e t) -> p c t e", e=2, t=PACK)
+            src = wf_raw[b][:].rearrange("p t (c e) -> p c t e", e=2)
+            for lo in (0, 128):
                 if lo in vector_halves:
-                    nc.vector.tensor_copy(dst[:, lo : lo + 64], src[:, lo : lo + 64])
+                    nc.vector.tensor_copy(dst[:, lo : lo + 128], src[:, lo : lo + 128])
                 else:
-                    nc.scalar.activation(dst[:, lo : lo + 64], src[:, lo : lo + 64], COPY)
+                    nc.scalar.activation(dst[:, lo : lo + 128], src[:, lo : lo + 128], COPY)
             return grouped
 
         def quantise(codes, planes, values):
@@ -158,29 +159,29 @@ def tile_list_interface_face_flux_kernel(
             for t in range(PACK):
                 acc = psum.tile([P, BANK], F32, name="acc", tag="acc")
                 own = slice(P * t, P * (t + 1))
-                for a in range(2):
-                    nc.tensor.matmul_mx(
-                        out=acc[:], lhsT=w1_codes[a][b][:, own].bitcast(FP8X4), lhsT_scale=w1_planes[a][b][:, own],
-                        rhs=v_codes[a][:, cols].bitcast(FP8X4), rhs_scale=v_planes[4 + 4 * a : P, cols],
-                        start=(a == 0), stop=False)
                 first = PASS * b + P * t
-                nc.tensor.matmul_mx(
-                    out=acc[:], lhsT=w4_codes[:, 2 * first : 2 * (first + P)].bitcast(FP4X4),
-                    lhsT_scale=w4_planes[:, first : first + P],
-                    rhs=v2_codes[:, cols].bitcast(FP8X4), rhs_scale=v2_planes[:, cols],
-                    start=False, stop=True)
-                nc.scalar.activation(diff[b][:, t, cols], acc[:], IDENTITY, bias=jump_sb[:, b, t : t + 1], scale=-1.0)
+                left = [(w1_codes[a][b][:, own].bitcast(FP8X4), w1_planes[a][b][:, own],
+                         v_codes[a][:, cols], v_planes[4 + 4 * a : P, cols]) for a in range(2)]
+                right = [(w4_codes[:, 2 * first : 2 * (first + P)].bitcast(FP4X4), w4_planes[:, first : first + P],
+                          v2_codes[:, cols], v2_planes[:, cols])]
+                passes = left + right if b == 0 else right + left
+                for n, (weights, weight_scales, states, state_scales) in enumerate(passes):
+                    nc.tensor.matmul_mx(
+                        out=acc[:], lhsT=weights, lhsT_scale=weight_scales, rhs=states.bitcast(FP8X4),
+                        rhs_scale=state_scales, start=(n == 0), stop=(n == len(passes) - 1))
+                nc.scalar.activation(diff[b][half][:, t, :], acc[:], IDENTITY, bias=jump_sb[:, b, t : t + 1], scale=-1.0)
 
         def form_h(b, lo, hi):
+            key = [c for c in cond_sb if c[0] == b and c[1] <= lo < c[2]][0]
             values = ring.tile([P, (hi - lo) * PACK], BF16, name="h_values", tag="h_values", bufs=3, align_bytes=64)
             nc.vector.tensor_tensor(
-                values[:].rearrange("p (c e t) -> p c t e", e=4, t=PACK),
-                diff[b][:, :, lo:hi].rearrange("p t (c e) -> p c t e", e=4),
-                cond_sb[b][:, :, lo:hi].rearrange("p t (c e) -> p c t e", e=4), MULT)
+                values[:].rearrange("p (c e t) -> p c t e", e=2, t=PACK),
+                diff[b][lo // BANK][:, :, lo % BANK : lo % BANK + hi - lo].rearrange("p t (c e) -> p c t e", e=2),
+                cond_sb[key][:, :, lo - key[1] : hi - key[1]].rearrange("p t (c e) -> p c t e", e=2), MULT)
             return values
 
         def flux(lo, hi, share):
-            staged = ring.tile([P, N // P, hi - lo], F32, name="staged", tag="wide", bufs=4, align_bytes=64)
+            staged = ring.tile([P, N // P, hi - lo], F32, name="staged", tag="wide", bufs=5, align_bytes=64)
             for m in range(N // P):
                 acc = psum.tile([P, hi - lo], F32, name="acc", tag="acc")
                 own = slice(P * m, P * (m + 1))
@@ -195,30 +196,29 @@ def tile_list_interface_face_flux_kernel(
                     nc.scalar.activation(staged[:, m, :], acc[:], IDENTITY, bias=q0_sb[:, m : m + 1], scale=1.0)
             nc.sync.dma_start(out[:, lo:hi].rearrange("(m p) j -> p m j", p=P), staged[:])
 
-        gather(v_codes[0][:], left_words[0], U32, left_list[:])
         nc.vector.tensor_copy(
             w4_codes[:].bitcast(U16).rearrange("p (b t m) -> p b m t", b=2, t=PACK),
             w4_raw[:].bitcast(U16).rearrange("p (b m t) -> p b m t", b=2, t=PACK))
+        grouped00 = round_w1(0, 0, [0])
+        quantise(w1_codes[0][0][:], w1_planes[0][0][:], grouped00[:])
+        grouped10 = round_w1(1, 0, [0])
+        gather(v_codes[0][:], left_words[0], U32, left_list[:])
+        quantise(w1_codes[1][0][:], w1_planes[1][0][:], grouped10[:])
         gather(v_planes[:], left_scales, U8, left_list[:])
         gather(v_codes[1][:], left_words[1], U32, left_list[:])
-        gather(v2_planes[:], right_scales, U8, right_list[:])
-        grouped00 = round_w1(0, 0, 0)
-        grouped10 = round_w1(1, 0, 0)
-        quantise(w1_codes[0][0][:], w1_planes[0][0][:], grouped00[:])
-        quantise(w1_codes[1][0][:], w1_planes[1][0][:], grouped10[:])
         nc.vector.tensor_copy(
             w4_planes[:].rearrange("p (b t m) -> p b m t", b=2, t=PACK),
             w4_raw_scales[:].bitcast(U8).rearrange("p (b m t) -> p b m t", b=2, t=PACK))
+        gather(v2_planes[:], right_scales, U8, right_list[:])
         for half in range(2):
             gather(v2_codes[:, BANK * half : BANK * (half + 1)], right_words, U32, right_list[:, 32 * half : 32 * (half + 1)])
         project(0, 0)
         project(0, 1)
-        grouped01 = round_w1(0, 1, 64)
-        grouped11 = round_w1(1, 1, P)
+        grouped01 = round_w1(0, 1, [0, 2])
+        grouped11 = round_w1(1, 1, [0, 2])
         quantise(w1_codes[0][1][:], w1_planes[0][1][:], grouped01[:])
         quantise(w1_codes[1][1][:], w1_planes[1][1][:], grouped11[:])
         project(1, 0)
-        wf_grouped = [round_wf(0, [0]), round_wf(1, [])]
         project(1, 1)
 
         order = [(0, 0), (0, 1), (1, 0), (1, 1)] + [(b, c) for c in range(2, len(CHUNKS)) for b in range(2)]
@@ -234,6 +234,7 @@ def tile_list_interface_face_flux_kernel(
                 if pb == 1:
                     done.append(pc)
             if step == 4:
+                wf_grouped = [round_wf(0, [0, 128]), round_wf(1, [])]
                 for wb in range(2):
                     for lo in (0, 256):
                         quantise(wf_codes[wb][:, lo : lo + 256], wf_planes[wb][:, lo : lo + 256],

@@ -106,9 +106,9 @@ def tile_list_interface_face_flux_kernel(
             nc.sync.dma_start(q0_sb[:], q0.rearrange("(m p) -> p m", p=P))
         load_w1(0, 0)
         load_left_scales()
-        load_words(left_words[1], tab_words[1])
-        load_scales(w4_raw_scales, w4_scales)
         load_scales(right_scales, tab2_scales)
+        load_scales(w4_raw_scales, w4_scales)
+        load_words(left_words[1], tab_words[1])
         load_w1(1, 0)
         load_words(right_words, tab2_words[0])
         load_w1(0, 1)
@@ -199,17 +199,17 @@ def tile_list_interface_face_flux_kernel(
         nc.vector.tensor_copy(
             w4_codes[:].bitcast(U16).rearrange("p (b t m) -> p b m t", b=2, t=PACK),
             w4_raw[:].bitcast(U16).rearrange("p (b m t) -> p b m t", b=2, t=PACK))
-        grouped00 = round_w1(0, 0, [0])
+        grouped00 = round_w1(0, 0, [])
         quantise(w1_codes[0][0][:], w1_planes[0][0][:], grouped00[:])
-        grouped10 = round_w1(1, 0, [0])
+        grouped10 = round_w1(1, 0, [])
         gather(v_codes[0][:], left_words[0], U32, left_list[:])
         quantise(w1_codes[1][0][:], w1_planes[1][0][:], grouped10[:])
         gather(v_planes[:], left_scales, U8, left_list[:])
+        gather(v2_planes[:], right_scales, U8, right_list[:])
         gather(v_codes[1][:], left_words[1], U32, left_list[:])
         nc.vector.tensor_copy(
             w4_planes[:].rearrange("p (b t m) -> p b m t", b=2, t=PACK),
             w4_raw_scales[:].bitcast(U8).rearrange("p (b m t) -> p b m t", b=2, t=PACK))
-        gather(v2_planes[:], right_scales, U8, right_list[:])
         for half in range(2):
             gather(v2_codes[:, BANK * half : BANK * (half + 1)], right_words, U32, right_list[:, 32 * half : 32 * (half + 1)])
         project(0, 0)

from contextlib import ExitStack

import concourse.mybir as mybir

K, K2, H, N, T, T2, S = 1024, 512, 1024, 512, 2048, 4096, 1024
FLOPS = 2 * S * (K * H + K2 * H + H * N)

F32 = mybir.dt.float32
BF16 = mybir.dt.bfloat16
I32 = mybir.dt.int32
U32 = mybir.dt.uint32
U16 = mybir.dt.uint16
U8 = mybir.dt.uint8
FP8X4 = mybir.dt.float8_e4m3fn_x4
FP4X4 = mybir.dt.float4_e2m1fn_x4
MULT = mybir.AluOpType.mult
ADD = mybir.AluOpType.add
COPY = mybir.ActivationFunctionType.Copy
IDENTITY = mybir.ActivationFunctionType.Identity

P = 128
PACK = 4
PASS = P * PACK
BANK = 512
CHUNKS = [(0, 256), (256, 512), (512, 768), (768, 896), (896, 1024)]
B0_CHUNKS = [(0, 256), (256, 512), (512, 768), (768, 1024)]


def tile_list_interface_face_flux_kernel(
    tc, tab_words, tab_scales, offs, tab2_words, tab2_scales, offs2,
    w1, w4_words, w4_scales, jump, cond, wf, q0, out,
):
    nc = tc.nc
    with ExitStack() as ctx:
        held = ctx.enter_context(tc.tile_pool(name="held", bufs=1))
        ring = ctx.enter_context(tc.tile_pool(name="ring", bufs=1))
        psum = ctx.enter_context(tc.psum_pool(name="psum", bufs=8))

        def keep(shape, dtype, name):
            return held.tile(shape, dtype, name=name, align_bytes=64)

        left_list = keep([P, S // 16], U16, "left_list")
        right_list = keep([P, S // 16], U16, "right_list")
        left_words = [keep([P, T], I32, f"left_words{a}") for a in range(2)]
        right_words = keep([P, T2], I32, "right_words")
        left_scales = keep([P, T // 4], I32, "left_scales")
        right_scales = keep([P, T2 // 4], I32, "right_scales")
        w4_raw = keep([P, H // 2], I32, "w4_raw")
        w4_raw_scales = keep([P, H // 4], I32, "w4_raw_scales")
        w4_codes = keep([P, 2 * H], U8, "w4_codes")
        w4_planes = keep([P, H], U8, "w4_planes")
        v_codes = [keep([P, S], U32, f"v_codes{a}") for a in range(2)]
        v_planes = keep([P, S], U8, "v_planes")
        v2_codes = keep([P, S], U32, "v2_codes")
        v2_planes = keep([P, S], U8, "v2_planes")
        w1_codes = [[keep([P, PASS], U32, f"w1_codes{a}{b}") for b in range(2)] for a in range(2)]
        w1_planes = [[keep([P, PASS], U8, f"w1_planes{a}{b}") for b in range(2)] for a in range(2)]
        wf_raw = [keep([P, PACK, N], F32, f"wf_raw{b}") for b in range(2)]
        wf_codes = [keep([P, N], U32, f"wf_codes{b}") for b in range(2)]
        wf_planes = [keep([P, N], U8, f"wf_planes{b}") for b in range(2)]
        diff = [[keep([P, PACK, BANK], F32, f"diff{b}{half}") for half in range(2)] for b in range(2)]
        cond_sb = {}
        h_codes = [keep([P, S], U32, f"h_codes{b}") for b in range(2)]
        h_planes = [keep([P, S], U8, f"h_planes{b}") for b in range(2)]
        jump_sb = keep([P, 2, PACK], F32, "jump_sb")
        q0_sb = keep([P, N // P], F32, "q0_sb")
        w1_raw = [[ring.tile([P, PACK, PASS], F32, name=f"w1_raw{a}{b}", tag="wide", bufs=5, align_bytes=64)
                   for b in range(2)] for a in range(2)]

        nc.gpsimd.memset(left_scales[:], 0)
        nc.vector.memset(right_scales[:], 0)
        nc.vector.memset(w4_raw_scales[:], 0)

        def load_left_scales():
            for quad in range(4):
                nc.sync.dma_start(left_scales[32 * quad + 4 : 32 * quad + 12, :],
                                  tab_scales[:, 4 * quad : 4 * quad + 4, :].bitcast(I32))

        def load_scales(dst, src):
            rows = src[0].bitcast(I32).rearrange("(q r) n -> r q n", r=4)
            for r in range(4):
                nc.sync.dma_start(dst[r:P:32, :], rows[r])

        def load_words(dst, src):
            nc.sync.dma_start(dst[:], src.rearrange("p n i -> p (n i)").bitcast(I32))

        def load_w1(a, b):
            rows = w1[PASS * a : PASS * (a + 1), PASS * b : PASS * (b + 1)]
            nc.sync.dma_start(w1_raw[a][b][:], rows.rearrange("(p i) c -> p i c", i=PACK))

        def load_cond(b, lo, hi):
            rows = cond[PASS * b : PASS * (b + 1), lo:hi]
            cond_sb[b, lo, hi] = keep([P, PACK, hi - lo], F32, f"cond{b}_{lo}")
            nc.sync.dma_start(cond_sb[b, lo, hi][:], rows.rearrange("(p t) j -> p t j", t=PACK))

        def load_wf(b):
            rows = wf[PASS * b : PASS * (b + 1), :]
            nc.sync.dma_start(wf_raw[b][:], rows.rearrange("(p t) n -> p t n", t=PACK))

        load_words(left_words[0], tab_words[0])
        nc.sync.dma_start(left_list[:], offs)
        nc.sync.dma_start(w4_raw[:], w4_words[0].bitcast(I32))
        nc.sync.dma_start(right_list[:], offs2)
        nc.sync.dma_start(jump_sb[:], jump.rearrange("(b p t) -> p b t", b=2, t=PACK))
        with nc.allow_non_contiguous_dma(reason="one value of q0 for each partition"):
            nc.sync.dma_start(q0_sb[:], q0.rearrange("(m p) -> p m", p=P))
        load_w1(0, 0)
        load_left_scales()
        load_scales(right_scales, tab2_scales)
        load_scales(w4_raw_scales, w4_scales)
        load_words(left_words[1], tab_words[1])
        load_w1(1, 0)
        load_words(right_words, tab2_words[0])
        load_w1(0, 1)
        load_w1(1, 1)
        load_cond(0, 0, 512)
        load_wf(0)
        load_cond(1, 0, 512)
        load_wf(1)
        load_cond(0, 512, 768)
        load_cond(1, 512, 768)
        load_cond(0, 768, 1024)
        load_cond(1, 768, 896)
        load_cond(1, 896, 1024)

        def staging(name):
            return ring.tile([P, PASS * PACK], BF16, name=name, tag="staging", bufs=3, align_bytes=64)

        def round_w1(a, b, vector_pairs):
            grouped = staging(f"w1_grouped{a}{b}")
            dst = grouped[:].rearrange("p (t m i) -> p m i t", t=PACK, i=PACK)
            src = w1_raw[a][b][:].rearrange("p i (m t) -> p m i t", t=PACK)
            for t in (0, 2):
                if t in vector_pairs:
                    nc.vector.tensor_scalar(dst[:, :, :, t : t + 2], src[:, :, :, t : t + 2], -1.0, None, MULT)
                else:
                    nc.scalar.activation(dst[:, :, :, t : t + 2], src[:, :, :, t : t + 2], COPY, scale=-1.0)
            return grouped

        def round_wf(b, vector_halves):
            grouped = staging(f"wf_grouped{b}")
            dst = grouped[:].rearrange("p (c e t) -> p c t e", e=2, t=PACK)
            src = wf_raw[b][:].rearrange("p t (c e) -> p c t e", e=2)
            for lo in (0, 128):
                if lo in vector_halves:
                    nc.vector.tensor_copy(dst[:, lo : lo + 128], src[:, lo : lo + 128])
                else:
                    nc.scalar.activation(dst[:, lo : lo + 128], src[:, lo : lo + 128], COPY)
            return grouped

        def quantise(codes, planes, values):
            nc.vector.quantize_mx(out=codes.bitcast(FP8X4), scales=planes, in_=values)

        def gather(dst, window, dtype, offsets):
            nc.vector.tensor_copy(dst, window[:].bitcast(dtype).indirect(offsets))

        def project(b, half):
            cols = slice(BANK * half, BANK * (half + 1))
            for t in range(PACK):
                acc = psum.tile([P, BANK], F32, name="acc", tag="acc")
                own = slice(P * t, P * (t + 1))
                first = PASS * b + P * t
                left = [(w1_codes[a][b][:, own].bitcast(FP8X4), w1_planes[a][b][:, own],
                         v_codes[a][:, cols], v_planes[4 + 4 * a : P, cols]) for a in range(2)]
                right = [(w4_codes[:, 2 * first : 2 * (first + P)].bitcast(FP4X4), w4_planes[:, first : first + P],
                          v2_codes[:, cols], v2_planes[:, cols])]
                passes = left + right if b == 0 else right + left
                for n, (weights, weight_scales, states, state_scales) in enumerate(passes):
                    nc.tensor.matmul_mx(
                        out=acc[:], lhsT=weights, lhsT_scale=weight_scales, rhs=states.bitcast(FP8X4),
                        rhs_scale=state_scales, start=(n == 0), stop=(n == len(passes) - 1))
                nc.scalar.activation(diff[b][half][:, t, :], acc[:], IDENTITY, bias=jump_sb[:, b, t : t + 1], scale=-1.0)

        def form_h(b, lo, hi):
            key = [c for c in cond_sb if c[0] == b and c[1] <= lo < c[2]][0]
            values = ring.tile([P, (hi - lo) * PACK], BF16, name="h_values", tag="h_values", bufs=3, align_bytes=64)
            nc.vector.tensor_tensor(
                values[:].rearrange("p (c e t) -> p c t e", e=2, t=PACK),
                diff[b][lo // BANK][:, :, lo % BANK : lo % BANK + hi - lo].rearrange("p t (c e) -> p c t e", e=2),
                cond_sb[key][:, :, lo - key[1] : hi - key[1]].rearrange("p t (c e) -> p c t e", e=2), MULT)
            return values

        def flux(lo, hi, share):
            staged = ring.tile([P, N // P, hi - lo], F32, name="staged", tag="wide", bufs=5, align_bytes=64)
            for m in range(N // P):
                acc = psum.tile([P, hi - lo], F32, name="acc", tag="acc")
                own = slice(P * m, P * (m + 1))
                for b in range(2):
                    nc.tensor.matmul_mx(
                        out=acc[:], lhsT=wf_codes[b][:, own].bitcast(FP8X4), lhsT_scale=wf_planes[b][:, own],
                        rhs=h_codes[b][:, lo:hi].bitcast(FP8X4), rhs_scale=h_planes[b][:, lo:hi],
                        start=(b == 0), stop=(b == 1))
                if share and m % 2 == 1:
                    nc.vector.tensor_scalar(staged[:, m, :], acc[:], q0_sb[:, m : m + 1], None, ADD)
                else:
                    nc.scalar.activation(staged[:, m, :], acc[:], IDENTITY, bias=q0_sb[:, m : m + 1], scale=1.0)
            nc.sync.dma_start(out[:, lo:hi].rearrange("(m p) j -> p m j", p=P), staged[:])

        nc.vector.tensor_copy(
            w4_codes[:].bitcast(U16).rearrange("p (b t m) -> p b m t", b=2, t=PACK),
            w4_raw[:].bitcast(U16).rearrange("p (b m t) -> p b m t", b=2, t=PACK))
        grouped00 = round_w1(0, 0, [])
        quantise(w1_codes[0][0][:], w1_planes[0][0][:], grouped00[:])
        grouped10 = round_w1(1, 0, [])
        gather(v_codes[0][:], left_words[0], U32, left_list[:])
        quantise(w1_codes[1][0][:], w1_planes[1][0][:], grouped10[:])
        gather(v_planes[:], left_scales, U8, left_list[:])
        gather(v2_planes[:], right_scales, U8, right_list[:])
        gather(v_codes[1][:], left_words[1], U32, left_list[:])
        nc.vector.tensor_copy(
            w4_planes[:].rearrange("p (b t m) -> p b m t", b=2, t=PACK),
            w4_raw_scales[:].bitcast(U8).rearrange("p (b m t) -> p b m t", b=2, t=PACK))
        for half in range(2):
            gather(v2_codes[:, BANK * half : BANK * (half + 1)], right_words, U32, right_list[:, 32 * half : 32 * (half + 1)])
        project(0, 0)
        project(0, 1)
        grouped01 = round_w1(0, 1, [0, 2])
        grouped11 = round_w1(1, 1, [0, 2])
        quantise(w1_codes[0][1][:], w1_planes[0][1][:], grouped01[:])
        quantise(w1_codes[1][1][:], w1_planes[1][1][:], grouped11[:])
        project(1, 0)
        project(1, 1)

        order = [(0, 0), (0, 1), (1, 0), (1, 1)] + [(b, c) for c in range(2, len(CHUNKS)) for b in range(2)]
        pending = None
        done = []
        for step, (b, c) in enumerate(order + [(None, None)]):
            if b is not None:
                values = form_h(b, *CHUNKS[c])
            if pending is not None:
                pb, pc, pv = pending
                lo, hi = CHUNKS[pc]
                quantise(h_codes[pb][:, lo:hi], h_planes[pb][:, lo:hi], pv[:])
                if pb == 1:
                    done.append(pc)
            if step == 4:
                wf_grouped = [round_wf(0, [0, 128]), round_wf(1, [])]
                for wb in range(2):
                    for lo in (0, 256):
                        quantise(wf_codes[wb][:, lo : lo + 256], wf_planes[wb][:, lo : lo + 256],
                                 wf_grouped[wb][:, PACK * lo : PACK * (lo + 256)])
            if step >= 4:
                for dc in done:
                    flux(*CHUNKS[dc], dc == len(CHUNKS) - 1)
                done = []
            pending = (b, c, values)
